import numpy as np
import ml_dtypes


def mxq(x, axis, fmt="e4m3"):
    dtype, down = {"e4m3": (ml_dtypes.float8_e4m3fn, 7), "e5m2": (ml_dtypes.float8_e5m2, 14)}[fmt]
    v = np.moveaxis(np.asarray(x, np.float32).astype(ml_dtypes.bfloat16).astype(np.float64), axis, -1)
    blocks = v.reshape(v.shape[:-1] + (-1, 32))
    amax = np.abs(blocks).max(-1, keepdims=True)
    byte = np.maximum(np.where(amax > 0, np.frexp(amax)[1] - 1 + 127, 0) - down, 1)
    scale = np.exp2(byte - 127.0)
    codes = (blocks / scale).astype(np.float32).astype(dtype).astype(np.float64)
    return np.moveaxis((codes * scale).reshape(v.shape), -1, axis)


WIDE = False


def mx_kscale(k):
    if not WIDE:
        return np.ones(k)
    levels = np.array([10, -10, 5, -5, 0])
    if k % 512:
        return np.exp2(np.random.permutation(np.resize(levels, k // 32))).repeat(32)
    a = np.empty((k // 512, 16))
    for p in range(k // 512):
        a[p, :8] = np.random.permutation(np.resize(levels, 8))
        for g in range(8):
            far = levels[np.abs(levels - a[p, g]) >= 10]
            a[p, g + 8] = far[np.random.randint(len(far))]
    return np.exp2(a.ravel()).repeat(32)


def f64(x):
    return np.asarray(x).astype(np.float64)


def striped(idx):
    return np.tile(idx.reshape(-1, 16).T, (8, 1)).astype(np.uint16)


def unstriped(offs):
    return offs[:16].T.reshape(-1).astype(np.int64)


E2M1 = np.array([0.0, 0.5, 1.0, 1.5, 2.0, 3.0, 4.0, 6.0, -0.0, -0.5, -1.0, -1.5, -2.0, -3.0, -4.0, -6.0])


def pack_weight(w, fmt):
    k, n = w.shape
    w = f64(np.asarray(w, np.float32).astype(ml_dtypes.bfloat16)).reshape(k // 32, 32, n)
    amax = np.abs(w).max(1)
    if fmt == "e4m3":
        byte = np.frexp(amax)[1] - 1 + 127 - 7
    else:
        mant, ex = np.frexp(amax / 6.0)
        byte = np.where(mant > 0.5, ex, ex - 1) + 127
    byte = np.clip(np.where(amax > 0, byte, 1), 1, 254)
    scaled = (w * np.exp2(127.0 - byte)[:, None, :]).reshape(k, n).astype(np.float32)
    by_word = np.ascontiguousarray(scaled.reshape(k // 512, 128, 4, n).transpose(0, 1, 3, 2))
    if fmt == "e4m3":
        words = by_word.astype(ml_dtypes.float8_e4m3fn).view(np.uint8)
    else:
        c = by_word.astype(ml_dtypes.float4_e2m1fn).view(np.uint8) & 0xF
        words = (c[..., 0::2] | (c[..., 1::2] << 4)).reshape(k // 512, 128, 2 * n)
    return np.ascontiguousarray(words), np.ascontiguousarray(byte.astype(np.uint8).reshape(k // 512, 16, n))


def unpack_weight(words, scales, fmt):
    g, _, n = scales.shape
    words = np.ascontiguousarray(words).reshape(g, 128, n, -1)
    if fmt == "e4m3":
        vals = words.view(ml_dtypes.float8_e4m3fn).astype(np.float64)
    else:
        nib = np.empty((g, 128, n, 4), np.uint8)
        nib[..., 0::2] = words & 0xF
        nib[..., 1::2] = words >> 4
        vals = E2M1[nib]
    vals = vals * np.repeat(np.exp2(scales.astype(np.float64) - 127.0), 8, axis=1)[..., None]
    return vals.transpose(0, 1, 3, 2).reshape(g * 512, n)


def gelu(v):
    return 0.5 * v * (1.0 + np.tanh(np.sqrt(2.0 / np.pi) * (v + 0.044715 * v**3)))


K, H, T, S, T2, P = 512, 1024, 4096, 1024, 2048, 1024

def setup_inputs():
    n = np.random.standard_normal
    s = mx_kscale(K)[:, None]
    u = mx_kscale(H)[:, None]
    tab_words, tab_scales = pack_weight(n((K, T)) * s, "e4m3")
    w3_words, w3_scales = pack_weight(0.7 * n((K, H)) * u.T / (s * np.sqrt(K)), "e2m1")
    return {
        "tab_words": tab_words, "tab_scales": tab_scales,
        "offs": striped(np.random.permutation(T)[:S]),
        "offs2": striped(np.random.permutation(T2)[:S]),
        "offs3": striped(np.random.permutation(T2)[:P]),
        "offs4": striped(np.random.permutation(T2)[:P]),
        "w1": (0.35 * n((K, H)) / (s * np.sqrt(K))).astype(np.float32),
        "phase": np.random.uniform(-1.2, 1.2, H).astype(np.float32),
        "gain": (2.2 * np.exp(0.3 * n(H)) * u[:, 0]).astype(np.float32),
        "page0": (n((H, T2)) * u).astype(np.float32),
        "wgs": np.exp(0.3 * n((128, S))).astype(np.float32),
        "ceil": ((n((H, P)) + 0.5) * u).astype(np.float32),
        "w2": (n((H, H)) * u.T / (u * np.sqrt(H))).astype(np.float32),
        "w3_words": w3_words, "w3_scales": w3_scales,
        "wgo": np.exp(0.3 * n((128, P))).astype(np.float32),
    }

def reference(tab_words, tab_scales, offs, offs2, offs3, offs4, w1, phase, gain,
              page0, wgs, ceil, w2, w3_words, w3_scales, wgo):
    v = unpack_weight(tab_words, tab_scales, "e4m3")[:, unstriped(offs)]
    w3 = unpack_weight(w3_words, w3_scales, "e2m1")
    e = mxq(f64(w1), 0, "e4m3").T @ v
    h = np.sin(e + f64(phase)[:, None]) * f64(gain)[:, None]
    page = f64(page0).copy()
    page[:, unstriped(offs2)] = np.tile(f64(wgs), (H // 128, 1)) * h
    x = np.minimum(page[:, unstriped(offs3)], f64(ceil))
    d = w3.T @ v
    y = (mxq(f64(w2), 0, "e4m3").T @ mxq(x, 0, "e4m3")) + d
    page[:, unstriped(offs4)] = np.tile(f64(wgo), (H // 128, 1)) * y
    return page

@@ -1,0 +1,358 @@
+import math
+from contextlib import ExitStack
+
+import concourse.mybir as mybir
+from concourse.masks import make_identity
+
+K, H, T, S, T2 = 512, 1024, 4096, 1024, 2048
+FLOPS = 2 * S * H * (K + H + K)
+
+F32 = mybir.dt.float32
+BF16 = mybir.dt.bfloat16
+I32 = mybir.dt.int32
+U32 = mybir.dt.uint32
+U16 = mybir.dt.uint16
+U8 = mybir.dt.uint8
+FP8X4 = mybir.dt.float8_e4m3fn_x4
+FP4X4 = mybir.dt.float4_e2m1fn_x4
+ACT = mybir.ActivationFunctionType
+ALU = mybir.AluOpType
+
+P = 128
+PACK = 4
+HALF = 512
+QUARTER = 256
+TILES = H // P
+PASSES = H // (P * PACK)
+X_LAG = 2
+LATE_TILES = (5, 6)
+
+
+def tile_list_discharge_joint_page_kernel(
+    tc, tab_words, tab_scales, offs, offs2, offs3, offs4, w1, phase, gain,
+    page0, wgs, ceil, w2, w3_words, w3_scales, wgo, out,
+):
+    nc = tc.nc
+    with ExitStack() as ctx:
+        keep = ctx.enter_context(tc.tile_pool(name="keep", bufs=1))
+        ring = ctx.enter_context(tc.tile_pool(name="ring", bufs=2))
+        psum = ctx.enter_context(tc.psum_pool(name="psum", bufs=1))
+
+        def kept(name, cols, dtype):
+            return keep.tile([P, cols], dtype, name=name, align_bytes=64)
+
+        def entries(offsets, j0, n):
+            return offsets[:, j0 // 16 : (j0 + n) // 16]
+
+        def cols(i, width):
+            return slice(i * width, (i + 1) * width)
+
+        banks = [psum.tile([P, HALF], F32, name="bank%d" % i) for i in range(8)]
+        sum_banks, turn_banks, back_banks, word_banks = banks[0:2], banks[2:4], banks[4:6], banks[6:8]
+
+        look_list = keep.tile([P, S // 16], U16, name="look_list")
+        put_list = keep.tile([P, S // 16], U16, name="put_list")
+        pick_list = keep.tile([P, S // 16], U16, name="pick_list")
+        final_list = keep.tile([P, S // 16], U16, name="final_list")
+        tab_w = kept("tab_w", T, I32)
+        tab_s = kept("tab_s", T, U8)
+        v_w = kept("v_w", S, U32)
+        v_s = kept("v_s", S, U8)
+        w3_w = kept("w3_w", 2 * H, U8)
+        w3_s = kept("w3_s", H, U8)
+        w1_w = kept("w1_w", H, U32)
+        w1_s = kept("w1_s", H, U8)
+        w2_w = kept("w2_w", PASSES * H, U32)
+        w2_s = kept("w2_s", PASSES * H, U8)
+        x_w = kept("x_w", PASSES * S, U32)
+        x_s = kept("x_s", PASSES * S, U8)
+        rounded = kept("rounded", PACK * H, BF16)
+        wgs_sb = kept("wgs_sb", S, F32)
+        wgo_sb = kept("wgo_sb", S, F32)
+        picked = kept("picked", S, F32)
+        rows = kept("rows", P, F32)
+        shift = kept("shift", TILES, F32)
+        gains = kept("gains", TILES, F32)
+        half_pi = kept("half_pi", 1, F32)
+        ident = kept("ident", P, F32)
+        ident_bf = kept("ident_bf", P, BF16)
+        pages = [kept("page%d" % m, T2, F32) for m in range(TILES)]
+
+        nc.vector.memset(tab_s[:].bitcast(I32), 0)
+        nc.gpsimd.memset(rows[:], 0.0)
+        make_identity(nc, ident[:])
+        make_identity(nc, ident_bf[:])
+
+        def load_scale_rows(queue, plane, scales):
+            for q in range(4):
+                queue.dma_start(
+                    out=plane[32 * q : 32 * q + 4, :].bitcast(I32),
+                    in_=scales[0, 4 * q : 4 * q + 4, :].bitcast(I32),
+                )
+
+        def load_weight(tile, rows_hbm):
+            nc.sync.dma_start(out=tile, in_=rows_hbm.rearrange("(p t) c -> p t c", t=PACK))
+
+        w1_first = keep.tile([P, PACK, QUARTER], F32, name="w1_first")
+        nc.sync.dma_start(look_list[:], offs)
+        load_weight(w1_first[:], w1[:, 0:QUARTER])
+        nc.sync.dma_start(out=tab_w[:], in_=tab_words[0].rearrange("p n t -> p (n t)").bitcast(I32))
+        nc.scalar.dma_start(out=rows[0:TILES, :], in_=phase.rearrange("(m p) -> m p", p=P))
+        nc.scalar.dma_start(out=rows[TILES : 2 * TILES, :], in_=gain.rearrange("(m p) -> m p", p=P))
+        load_scale_rows(nc.gpsimd, tab_s, tab_scales)
+        nc.sync.dma_start(put_list[:], offs2)
+        nc.sync.dma_start(out=wgs_sb[:], in_=wgs)
+        nc.sync.dma_start(out=pages[0][:], in_=page0[cols(0, P), :])
+        w1_next = ring.tile([P, PACK, QUARTER], F32, name="w1_next", tag="raw")
+        load_weight(w1_next[:], w1[:, QUARTER:HALF])
+        nc.sync.dma_start(pick_list[:], offs3)
+        ceils = {}
+
+        def load_ceil(m):
+            ceils[m] = ring.tile([P, S], F32, name="ceil_sb", tag="ceil", bufs=3)
+            nc.sync.dma_start(out=ceils[m][:], in_=ceil[cols(m, P), :])
+
+        load_ceil(0)
+        nc.sync.dma_start(out=pages[1][:], in_=page0[cols(1, P), :])
+        w1_last = ring.tile([P, PACK, HALF], F32, name="w1_last", tag="raw")
+        load_weight(w1_last[:], w1[:, HALF:H])
+        for m in range(2, TILES):
+            if m < 4:
+                load_ceil(m - 1)
+            nc.sync.dma_start(out=pages[m][:], in_=page0[cols(m, P), :])
+        nc.sync.dma_start(out=w3_w[:].bitcast(I32), in_=w3_words[0].bitcast(I32))
+        nc.sync.dma_start(final_list[:], offs4)
+        nc.sync.dma_start(out=wgo_sb[:], in_=wgo)
+
+        nc.tensor.transpose(banks[7][:, 0:P], rows[:], ident[:])
+        nc.scalar.activation(shift[:], banks[7][:, 0:TILES], ACT.Copy, bias=-math.pi / 2)
+        nc.scalar.activation(
+            half_pi[:], banks[7][:, 2 * TILES : 2 * TILES + 1], ACT.Copy, bias=math.pi / 2
+        )
+        nc.scalar.copy(gains[:], banks[7][:, TILES : 2 * TILES])
+
+        def round_weight(slot, raw):
+            nc.scalar.copy(
+                rounded[:, cols(slot, HALF)].rearrange("p (c i t) -> p c t i", i=4, t=PACK),
+                raw.rearrange("p t (c i) -> p c t i", i=4),
+            )
+
+        def quantise_w1(m):
+            if m < 2:
+                raw = w1_first[:, :, cols(m, P)]
+            elif m < 4:
+                raw = w1_next[:, :, cols(m - 2, P)]
+            else:
+                raw = w1_last[:, :, cols(m - 4, P)]
+            round_weight(m, raw)
+            nc.vector.quantize_mx(
+                out=w1_w[:, cols(m, P)].bitcast(FP8X4),
+                scales=w1_s[:, cols(m, P)],
+                in_=rounded[:, cols(m, HALF)],
+            )
+
+        w2_raw = {}
+
+        def load_w2(pair):
+            w2_raw[pair] = ring.tile([P, PASSES, PACK, QUARTER], F32, name="w2_raw", tag="raw")
+            for b in range(PASSES):
+                load_weight(w2_raw[pair][:, b], w2[cols(b, HALF), cols(pair, QUARTER)])
+
+        def quantise_w2(n):
+            slot = PASSES * (n % 4)
+            for b in range(PASSES):
+                round_weight(slot + b, w2_raw[n // 2][:, b, :, cols(n % 2, P)])
+            nc.vector.quantize_mx(
+                out=w2_w[:, cols(n, PASSES * P)].bitcast(FP8X4),
+                scales=w2_s[:, cols(n, PASSES * P)],
+                in_=rounded[:, slot * HALF : (slot + PASSES) * HALF],
+            )
+
+        def look_up_words(j0, n):
+            nc.vector.tensor_copy(
+                v_w[:, j0 : j0 + n], tab_w[:].bitcast(U32).indirect(entries(look_list, j0, n))
+            )
+
+        def look_up_scales(j0, n):
+            nc.vector.tensor_copy(v_s[:, j0 : j0 + n], tab_s[:].indirect(entries(look_list, j0, n)))
+
+        quantise_w1(0)
+        quantise_w1(1)
+        look_up_scales(0, HALF)
+        look_up_words(0, QUARTER)
+        look_up_words(QUARTER, QUARTER)
+        look_up_scales(HALF, HALF)
+        look_up_words(HALF, HALF)
+        nc.vector.memset(w3_s[:].bitcast(I32), 0)
+        load_scale_rows(nc.sync, w3_s, w3_scales)
+
+        pieces = [(0, j0, QUARTER) for j0 in range(0, S, QUARTER)]
+        pieces = pieces + [(m, j0, HALF) for m in range(1, TILES) for j0 in (0, HALF)]
+        folded, turns, h_tiles, x_rows, x_turned = {}, {}, {}, {}, {}
+
+        def stage_product(i):
+            m, j0, n = pieces[i]
+            e = sum_banks[i % 2][:, 0:n]
+            nc.tensor.matmul_mx(
+                out=e,
+                lhsT=w1_w[:, cols(m, P)].bitcast(FP8X4),
+                lhsT_scale=w1_s[:, cols(m, P)],
+                rhs=v_w[:, j0 : j0 + n].bitcast(FP8X4),
+                rhs_scale=v_s[:, j0 : j0 + n],
+                start=True,
+                stop=True,
+            )
+            folded[i] = ring.tile([P, HALF], F32, name="folded", tag="folded")
+            count = ring.tile([P, HALF], U32, name="count", tag="count")
+            turns[i] = ring.tile([P, HALF], F32, name="turns", tag="turns")
+            nc.scalar.activation(folded[i][:, 0:n], e, ACT.Abs, bias=shift[:, m : m + 1])
+            nc.scalar.activation(count[:, 0:n], folded[i][:, 0:n], ACT.Copy, scale=1.0 / (2 * math.pi))
+            nc.scalar.activation(turns[i][:, 0:n], count[:, 0:n], ACT.Copy, scale=-2 * math.pi)
+
+        def stage_reduce(i):
+            m, j0, n = pieces[i]
+            bank = turn_banks[i % 2]
+            for blk in range(n // P):
+                for src, first in ((folded[i], True), (turns[i], False)):
+                    nc.tensor.matmul(
+                        bank[:, cols(blk, P)], lhsT=src[:, cols(blk, P)], rhs=ident[:],
+                        is_transpose=True, start=first, stop=not first,
+                    )
+            folded[i] = ring.tile([P, HALF], F32, name="reduced", tag="reduced")
+            nc.scalar.activation(folded[i][:, 0:n], bank[:, 0:n], ACT.Abs)
+
+        def stage_sine(i):
+            m, j0, n = pieces[i]
+            bank = back_banks[i % 2]
+            for blk in range(n // P):
+                nc.tensor.transpose(bank[:, cols(blk, P)], folded[i][:, cols(blk, P)], ident[:])
+            sine = ring.tile([P, HALF], F32, name="sine", tag="sine")
+            nc.scalar.activation(sine[:, 0:n], bank[:, 0:n], ACT.Sin, bias=half_pi[:], scale=-1.0)
+            if j0 == 0:
+                h_tiles[m] = ring.tile([P, S], F32, name="h", tag="h", bufs=3)
+            nc.scalar.activation(
+                h_tiles[m][:, j0 : j0 + n], sine[:, 0:n], ACT.Copy, scale=gains[:, m : m + 1]
+            )
+
+        def put(m, offsets, j0, n, values, factors):
+            nc.vector.tensor_tensor(
+                pages[m][:].indirect(entries(offsets, j0, n)), values, factors[:, j0 : j0 + n], ALU.mult
+            )
+
+        def pick(m, half, slot):
+            nc.vector.tensor_copy(
+                picked[:, cols(slot, HALF)], pages[m][:].indirect(entries(pick_list, half * HALF, HALF))
+            )
+
+        def cap(m, half, slot):
+            x_rows[m, half] = ring.tile([P, HALF], BF16, name="x_rows", tag="x_rows", bufs=6)
+            nc.vector.tensor_tensor(
+                x_rows[m, half][:], picked[:, cols(slot, HALF)], ceils[m][:, cols(half, HALF)], ALU.min
+            )
+
+        def turn_x(m, half):
+            bank = back_banks[1]
+            b, q = divmod(m, 4)
+            for jb in range(4):
+                nc.tensor.transpose(
+                    bank[:].bitcast(BF16)[:, cols(jb, P)], x_rows[m, half][:, cols(jb, P)], ident_bf[:]
+                )
+            if q == 0:
+                x_turned[half, b] = ring.tile([P, 4, 2, P], F32, name="x_turned", tag="x_turned", bufs=3)
+            nc.scalar.copy(
+                x_turned[half, b][:, :, :, cols(q, 32)],
+                bank[:, 0:QUARTER].rearrange("j (b p u) -> j b u p", b=4, u=2),
+            )
+            if q == 3:
+                quantise_x(half, b)
+
+        def quantise_x(half, b):
+            grouped = ring.tile([P, 2 * HALF], F32, name="grouped", tag="grouped", align_bytes=64)
+            for pair in range(2):
+                bank = word_banks[pair]
+                for jj in range(2):
+                    for u in range(2):
+                        nc.tensor.transpose(
+                            bank[:, cols(2 * jj + u, P)], x_turned[half, b][:, 2 * pair + jj, u, :], ident[:]
+                        )
+                nc.scalar.copy(
+                    grouped[:, cols(pair, HALF)].rearrange("p (a j u) -> p a j u", a=2, u=2),
+                    bank[:].rearrange("p (a u j) -> p a j u", a=2, u=2),
+                )
+            span = cols(PASSES * b + half, HALF)
+            nc.vector.quantize_mx(
+                out=x_w[:, span].bitcast(FP8X4), scales=x_s[:, span], in_=grouped[:].bitcast(BF16)
+            )
+
+        for i, (m, j0, n) in enumerate(pieces):
+            if j0 == HALF and m + 2 < TILES:
+                quantise_w1(m + 2)
+            stage_product(i)
+            stage_reduce(i)
+            stage_sine(i)
+            if m == 0:
+                put(m, put_list, j0, n, h_tiles[m][:, j0 : j0 + n], wgs_sb)
+            if j0 + n == S:
+                if m > 0:
+                    put(m, put_list, 0, S, h_tiles[m][:], wgs_sb)
+                halves = (0,) if m in LATE_TILES else (0, 1)
+                for half in halves:
+                    pick(m, half, half)
+                for half in halves:
+                    cap(m, half, half)
+                if m + 3 < TILES:
+                    load_ceil(m + 3)
+                if m in (3, 5):
+                    load_w2(m // 2 - 1)
+                if m >= 6:
+                    quantise_w2(m - 6)
+                if m >= X_LAG:
+                    done = m - X_LAG
+                    for half in (0,) if done in LATE_TILES else (0, 1):
+                        turn_x(done, half)
+        for m in range(TILES - X_LAG, TILES):
+            turn_x(m, 0)
+        for slot, m in enumerate(LATE_TILES):
+            pick(m, 1, slot)
+        for slot, m in enumerate(LATE_TILES):
+            cap(m, 1, slot)
+
+        def second_stage(n, half):
+            bank = sum_banks[n % 2]
+            js = cols(half, HALF)
+            nc.tensor.matmul_mx(
+                out=bank[:],
+                lhsT=w3_w[:, cols(n, 2 * P)].bitcast(FP4X4),
+                lhsT_scale=w3_s[:, cols(n, P)],
+                rhs=v_w[:, js].bitcast(FP8X4),
+                rhs_scale=v_s[:, js],
+                start=True,
+                stop=False,
+            )
+            for b in range(PASSES):
+                span = cols(PASSES * b + half, HALF)
+                nc.tensor.matmul_mx(
+                    out=bank[:],
+                    lhsT=w2_w[:, cols(PASSES * n + b, P)].bitcast(FP8X4),
+                    lhsT_scale=w2_s[:, cols(PASSES * n + b, P)],
+                    rhs=x_w[:, span].bitcast(FP8X4),
+                    rhs_scale=x_s[:, span],
+                    start=False,
+                    stop=b == PASSES - 1,
+                )
+            y = ring.tile([P, HALF], F32, name="y", tag="y", bufs=3)
+            nc.scalar.copy(y[:], bank[:])
+            put(n, final_list, half * HALF, HALF, y[:], wgo_sb)
+
+        for n in range(TILES):
+            second_stage(n, 0)
+            if n == 0:
+                for m in LATE_TILES + (TILES - 1,):
+                    turn_x(m, 1)
+            if n % 2 == 0 and n // 2 + 2 < TILES // 2:
+                load_w2(n // 2 + 2)
+            if n + 2 < TILES:
+                quantise_w2(n + 2)
+        for n in range(TILES):
+            second_stage(n, 1)
+            nc.sync.dma_start(out=out[cols(n, P), :], in_=pages[n][:])

@@ -24,6 +24,7 @@ HALF = 512
 QUARTER = 256
 TILES = H // P
 PASSES = H // (P * PACK)
+FIRST_PIECES = 3
 X_LAG = 2
 LATE_TILES = (5, 6)
 
@@ -56,7 +57,7 @@ def tile_list_discharge_joint_page_kernel(
         final_list = keep.tile([P, S // 16], U16, name="final_list")
         tab_w = kept("tab_w", T, I32)
         tab_s = kept("tab_s", T, U8)
-        v_w = kept("v_w", S, U32)
+        v_w = {0: kept("v_w0", HALF, U32)}
         v_s = kept("v_s", S, U8)
         w3_w = kept("w3_w", 2 * H, U8)
         w3_s = kept("w3_s", H, U8)
@@ -83,9 +84,9 @@ def tile_list_discharge_joint_page_kernel(
         make_identity(nc, ident[:])
         make_identity(nc, ident_bf[:])
 
-        def load_scale_rows(queue, plane, scales):
+        def load_scale_rows(plane, scales):
             for q in range(4):
-                queue.dma_start(
+                nc.sync.dma_start(
                     out=plane[32 * q : 32 * q + 4, :].bitcast(I32),
                     in_=scales[0, 4 * q : 4 * q + 4, :].bitcast(I32),
                 )
@@ -93,18 +94,30 @@ def tile_list_discharge_joint_page_kernel(
         def load_weight(tile, rows_hbm):
             nc.sync.dma_start(out=tile, in_=rows_hbm.rearrange("(p t) c -> p t c", t=PACK))
 
-        w1_first = keep.tile([P, PACK, QUARTER], F32, name="w1_first")
+        vectors = keep.tile([2 * TILES, P], F32, name="vectors")
+        nc.sync.dma_start(out=vectors[0:TILES, :], in_=phase.rearrange("(m p) -> m p", p=P))
+        nc.sync.dma_start(out=vectors[TILES : 2 * TILES, :], in_=gain.rearrange("(m p) -> m p", p=P))
+        landed = ring.tile([P, 2, T // 4], I32, name="landed", tag="raw")
+        for upper in range(2):
+            nc.sync.dma_start(
+                out=landed[64 * upper : 64 * upper + 4],
+                in_=tab_scales[0, 8 * upper : 8 * upper + 8, :].bitcast(I32).rearrange("(q r) n -> r q n", q=2),
+            )
         nc.sync.dma_start(look_list[:], offs)
+        w1_first = keep.tile([P, PACK, QUARTER], F32, name="w1_first")
         load_weight(w1_first[:], w1[:, 0:QUARTER])
         nc.sync.dma_start(out=tab_w[:], in_=tab_words[0].rearrange("p n t -> p (n t)").bitcast(I32))
-        nc.scalar.dma_start(out=rows[0:TILES, :], in_=phase.rearrange("(m p) -> m p", p=P))
-        nc.scalar.dma_start(out=rows[TILES : 2 * TILES, :], in_=gain.rearrange("(m p) -> m p", p=P))
-        load_scale_rows(nc.gpsimd, tab_s, tab_scales)
         nc.sync.dma_start(put_list[:], offs2)
-        nc.sync.dma_start(out=wgs_sb[:], in_=wgs)
-        nc.sync.dma_start(out=pages[0][:], in_=page0[cols(0, P), :])
+        nc.scalar.copy(rows[0 : 2 * TILES, :], vectors[:])
+        for q in range(4):
+            upper, side = divmod(q, 2)
+            nc.vector.tensor_copy(
+                tab_s[32 * q : 32 * q + 4, :].bitcast(I32), landed[64 * upper : 64 * upper + 4, side, :]
+            )
         w1_next = ring.tile([P, PACK, QUARTER], F32, name="w1_next", tag="raw")
         load_weight(w1_next[:], w1[:, QUARTER:HALF])
+        nc.sync.dma_start(out=wgs_sb[:], in_=wgs)
+        nc.sync.dma_start(out=pages[0][:], in_=page0[cols(0, P), :])
         nc.sync.dma_start(pick_list[:], offs3)
         ceils = {}
 
@@ -125,11 +138,9 @@ def tile_list_discharge_joint_page_kernel(
         nc.sync.dma_start(out=wgo_sb[:], in_=wgo)
 
         nc.tensor.transpose(banks[7][:, 0:P], rows[:], ident[:])
-        nc.scalar.activation(shift[:], banks[7][:, 0:TILES], ACT.Copy, bias=-math.pi / 2)
-        nc.scalar.activation(
-            half_pi[:], banks[7][:, 2 * TILES : 2 * TILES + 1], ACT.Copy, bias=math.pi / 2
-        )
-        nc.scalar.copy(gains[:], banks[7][:, TILES : 2 * TILES])
+        nc.vector.tensor_scalar_add(shift[:], banks[7][:, 0:TILES], -math.pi / 2)
+        nc.vector.tensor_scalar_add(half_pi[:], banks[7][:, 2 * TILES : 2 * TILES + 1], math.pi / 2)
+        nc.vector.tensor_copy(gains[:], banks[7][:, TILES : 2 * TILES])
 
         def round_weight(slot, raw):
             nc.scalar.copy(
@@ -168,71 +179,89 @@ def tile_list_discharge_joint_page_kernel(
                 in_=rounded[:, slot * HALF : (slot + PASSES) * HALF],
             )
 
+        def words_of(j0, n):
+            return v_w[j0 // HALF][:, j0 % HALF : j0 % HALF + n]
+
         def look_up_words(j0, n):
             nc.vector.tensor_copy(
-                v_w[:, j0 : j0 + n], tab_w[:].bitcast(U32).indirect(entries(look_list, j0, n))
+                words_of(j0, n), tab_w[:].bitcast(U32).indirect(entries(look_list, j0, n))
             )
 
         def look_up_scales(j0, n):
             nc.vector.tensor_copy(v_s[:, j0 : j0 + n], tab_s[:].indirect(entries(look_list, j0, n)))
 
-        quantise_w1(0)
-        quantise_w1(1)
-        look_up_scales(0, HALF)
-        look_up_words(0, QUARTER)
-        look_up_words(QUARTER, QUARTER)
-        look_up_scales(HALF, HALF)
-        look_up_words(HALF, HALF)
-        nc.vector.memset(w3_s[:].bitcast(I32), 0)
-        load_scale_rows(nc.sync, w3_s, w3_scales)
-
-        pieces = [(0, j0, QUARTER) for j0 in range(0, S, QUARTER)]
+        pieces = [(0, 0, QUARTER), (0, QUARTER, QUARTER), (0, HALF, HALF)]
         pieces = pieces + [(m, j0, HALF) for m in range(1, TILES) for j0 in (0, HALF)]
-        folded, turns, h_tiles, x_rows, x_turned = {}, {}, {}, {}, {}
+        folded = kept("folded", 2 * HALF, F32)
+        turns, reduced, h_tiles, x_rows, x_turned = {}, {}, {}, {}, {}
 
-        def stage_product(i):
+        def first_product(i):
             m, j0, n = pieces[i]
             e = sum_banks[i % 2][:, 0:n]
             nc.tensor.matmul_mx(
                 out=e,
                 lhsT=w1_w[:, cols(m, P)].bitcast(FP8X4),
                 lhsT_scale=w1_s[:, cols(m, P)],
-                rhs=v_w[:, j0 : j0 + n].bitcast(FP8X4),
+                rhs=words_of(j0, n).bitcast(FP8X4),
                 rhs_scale=v_s[:, j0 : j0 + n],
                 start=True,
                 stop=True,
             )
-            folded[i] = ring.tile([P, HALF], F32, name="folded", tag="folded")
-            count = ring.tile([P, HALF], U32, name="count", tag="count")
-            turns[i] = ring.tile([P, HALF], F32, name="turns", tag="turns")
-            nc.scalar.activation(folded[i][:, 0:n], e, ACT.Abs, bias=shift[:, m : m + 1])
-            nc.scalar.activation(count[:, 0:n], folded[i][:, 0:n], ACT.Copy, scale=1.0 / (2 * math.pi))
-            nc.scalar.activation(turns[i][:, 0:n], count[:, 0:n], ACT.Copy, scale=-2 * math.pi)
+            return e
 
-        def stage_reduce(i):
+        def sine_and_gain(i, angle):
             m, j0, n = pieces[i]
-            bank = turn_banks[i % 2]
-            for blk in range(n // P):
-                for src, first in ((folded[i], True), (turns[i], False)):
-                    nc.tensor.matmul(
-                        bank[:, cols(blk, P)], lhsT=src[:, cols(blk, P)], rhs=ident[:],
-                        is_transpose=True, start=first, stop=not first,
-                    )
-            folded[i] = ring.tile([P, HALF], F32, name="reduced", tag="reduced")
-            nc.scalar.activation(folded[i][:, 0:n], bank[:, 0:n], ACT.Abs)
-
-        def stage_sine(i):
-            m, j0, n = pieces[i]
-            bank = back_banks[i % 2]
-            for blk in range(n // P):
-                nc.tensor.transpose(bank[:, cols(blk, P)], folded[i][:, cols(blk, P)], ident[:])
             sine = ring.tile([P, HALF], F32, name="sine", tag="sine")
-            nc.scalar.activation(sine[:, 0:n], bank[:, 0:n], ACT.Sin, bias=half_pi[:], scale=-1.0)
+            nc.scalar.activation(sine[:, 0:n], angle, ACT.Sin, bias=half_pi[:], scale=-1.0)
             if j0 == 0:
                 h_tiles[m] = ring.tile([P, S], F32, name="h", tag="h", bufs=3)
             nc.scalar.activation(
                 h_tiles[m][:, j0 : j0 + n], sine[:, 0:n], ACT.Copy, scale=gains[:, m : m + 1]
             )
+
+        def reduce_on_vector(i):
+            m, j0, n = pieces[i]
+            e = first_product(i)
+            if i == 0:
+                count = keep.tile([P, HALF], I32, name="first_count", tag="v_w1", align_bytes=64)[:, 0:n]
+            else:
+                count = ring.tile([P, HALF], I32, name="signed_count", tag="count")[:, 0:n]
+            rest = ring.tile([P, HALF], F32, name="rest", tag="turns")[:, 0:n]
+            size = folded[:, 0:n]
+            nc.vector.tensor_scalar(count, e, shift[:, m : m + 1], 1.0 / (2 * math.pi), ALU.add, ALU.mult)
+            nc.vector.scalar_tensor_tensor(rest, count, -2 * math.pi, e, ALU.mult, ALU.add)
+            nc.scalar.activation(size, rest, ACT.Abs, bias=shift[:, m : m + 1])
+            sine_and_gain(i, size)
+
+        def stage_count(i):
+            m, j0, n = pieces[i]
+            e = first_product(i)
+            size = folded[:, (i % 2) * HALF : (i % 2) * HALF + n]
+            count = ring.tile([P, HALF], U32, name="count", tag="count")
+            turns[i] = ring.tile([P, HALF], F32, name="turns", tag="turns")
+            nc.scalar.activation(size, e, ACT.Abs, bias=shift[:, m : m + 1])
+            nc.scalar.activation(count[:, 0:n], size, ACT.Copy, scale=1.0 / (2 * math.pi))
+            nc.scalar.activation(turns[i][:, 0:n], count[:, 0:n], ACT.Copy, scale=-2 * math.pi)
+
+        def stage_reduce(i):
+            m, j0, n = pieces[i]
+            bank = turn_banks[i % 2]
+            size = folded[:, (i % 2) * HALF : (i % 2) * HALF + n]
+            for blk in range(n // P):
+                for src, first in ((size, True), (turns[i], False)):
+                    nc.tensor.matmul(
+                        bank[:, cols(blk, P)], lhsT=src[:, cols(blk, P)], rhs=ident[:],
+                        is_transpose=True, start=first, stop=not first,
+                    )
+            reduced[i] = ring.tile([P, HALF], F32, name="reduced", tag="reduced")
+            nc.scalar.activation(reduced[i][:, 0:n], bank[:, 0:n], ACT.Abs)
+
+        def stage_sine(i):
+            m, j0, n = pieces[i]
+            bank = back_banks[i % 2]
+            for blk in range(n // P):
+                nc.tensor.transpose(bank[:, cols(blk, P)], reduced[i][:, cols(blk, P)], ident[:])
+            sine_and_gain(i, bank[:, 0:n])
 
         def put(m, offsets, j0, n, values, factors):
             nc.vector.tensor_tensor(
@@ -251,7 +280,7 @@ def tile_list_discharge_joint_page_kernel(
             )
 
         def turn_x(m, half):
-            bank = back_banks[1]
+            bank = back_banks[0]
             b, q = divmod(m, 4)
             for jb in range(4):
                 nc.tensor.transpose(
@@ -284,32 +313,55 @@ def tile_list_discharge_joint_page_kernel(
                 out=x_w[:, span].bitcast(FP8X4), scales=x_s[:, span], in_=grouped[:].bitcast(BF16)
             )
 
-        for i, (m, j0, n) in enumerate(pieces):
-            if j0 == HALF and m + 2 < TILES:
-                quantise_w1(m + 2)
-            stage_product(i)
-            stage_reduce(i)
-            stage_sine(i)
+        def finish_piece(i):
+            m, j0, n = pieces[i]
             if m == 0:
                 put(m, put_list, j0, n, h_tiles[m][:, j0 : j0 + n], wgs_sb)
-            if j0 + n == S:
-                if m > 0:
-                    put(m, put_list, 0, S, h_tiles[m][:], wgs_sb)
-                halves = (0,) if m in LATE_TILES else (0, 1)
-                for half in halves:
-                    pick(m, half, half)
-                for half in halves:
-                    cap(m, half, half)
-                if m + 3 < TILES:
-                    load_ceil(m + 3)
-                if m in (3, 5):
-                    load_w2(m // 2 - 1)
-                if m >= 6:
-                    quantise_w2(m - 6)
-                if m >= X_LAG:
-                    done = m - X_LAG
-                    for half in (0,) if done in LATE_TILES else (0, 1):
-                        turn_x(done, half)
+            if j0 + n < S:
+                return
+            if m > 0:
+                put(m, put_list, 0, S, h_tiles[m][:], wgs_sb)
+            halves = (0,) if m in LATE_TILES else (0, 1)
+            for half in halves:
+                pick(m, half, half)
+            for half in halves:
+                cap(m, half, half)
+            if m + 3 < TILES:
+                load_ceil(m + 3)
+            if m in (3, 5):
+                load_w2(m // 2 - 1)
+            if m >= 6:
+                quantise_w2(m - 6)
+            if m >= X_LAG:
+                done = m - X_LAG
+                for half in (0,) if done in LATE_TILES else (0, 1):
+                    turn_x(done, half)
+
+        quantise_w1(0)
+        quantise_w1(1)
+        look_up_scales(0, HALF)
+        look_up_scales(HALF, HALF)
+        for i in range(FIRST_PIECES):
+            if pieces[i][1] == HALF:
+                v_w[1] = keep.tile([P, HALF], U32, name="v_w1", tag="v_w1", align_bytes=64)
+            look_up_words(pieces[i][1], pieces[i][2])
+            reduce_on_vector(i)
+        quantise_w1(2)
+        for i in range(FIRST_PIECES):
+            finish_piece(i)
+        nc.vector.memset(w3_s[:].bitcast(I32), 0)
+        load_scale_rows(w3_s, w3_scales)
+        for step in range(FIRST_PIECES, len(pieces) + 2):
+            if step < len(pieces):
+                m, j0, n = pieces[step]
+                if j0 == 0 and m + 2 < TILES:
+                    quantise_w1(m + 2)
+                stage_count(step)
+            if FIRST_PIECES <= step - 1 < len(pieces):
+                stage_reduce(step - 1)
+            if FIRST_PIECES <= step - 2:
+                stage_sine(step - 2)
+                finish_piece(step - 2)
         for m in range(TILES - X_LAG, TILES):
             turn_x(m, 0)
         for slot, m in enumerate(LATE_TILES):
@@ -324,7 +376,7 @@ def tile_list_discharge_joint_page_kernel(
                 out=bank[:],
                 lhsT=w3_w[:, cols(n, 2 * P)].bitcast(FP4X4),
                 lhsT_scale=w3_s[:, cols(n, P)],
-                rhs=v_w[:, js].bitcast(FP8X4),
+                rhs=v_w[half][:].bitcast(FP8X4),
                 rhs_scale=v_s[:, js],
                 start=True,
                 stop=False,

@@ -25,8 +25,11 @@ QUARTER = 256
 TILES = H // P
 PASSES = H // (P * PACK)
 FIRST_PIECES = 3
-X_LAG = 2
+PIPELINE_FROM = FIRST_PIECES + 2
+X_LAG = 3
+SLOTS = X_LAG + 1
 LATE_TILES = (5, 6)
+SPLIT_TILES = 2
 
 
 def tile_list_discharge_joint_page_kernel(
@@ -58,7 +61,7 @@ def tile_list_discharge_joint_page_kernel(
         tab_w = kept("tab_w", T, I32)
         tab_s = kept("tab_s", T, U8)
         v_w = {0: kept("v_w0", HALF, U32)}
-        v_s = kept("v_s", S, U8)
+        v_s = {0: kept("v_s0", HALF, U8)}
         w3_w = kept("w3_w", 2 * H, U8)
         w3_s = kept("w3_s", H, U8)
         w1_w = kept("w1_w", H, U32)
@@ -70,7 +73,7 @@ def tile_list_discharge_joint_page_kernel(
         rounded = kept("rounded", PACK * H, BF16)
         wgs_sb = kept("wgs_sb", S, F32)
         wgo_sb = kept("wgo_sb", S, F32)
-        picked = kept("picked", S, F32)
+        picked = kept("picked", 2 * S, F32)
         rows = kept("rows", P, F32)
         shift = kept("shift", TILES, F32)
         gains = kept("gains", TILES, F32)
@@ -179,16 +182,16 @@ def tile_list_discharge_joint_page_kernel(
                 in_=rounded[:, slot * HALF : (slot + PASSES) * HALF],
             )
 
-        def words_of(j0, n):
-            return v_w[j0 // HALF][:, j0 % HALF : j0 % HALF + n]
+        def within_half(halves, j0, n):
+            return halves[j0 // HALF][:, j0 % HALF : j0 % HALF + n]
 
         def look_up_words(j0, n):
             nc.vector.tensor_copy(
-                words_of(j0, n), tab_w[:].bitcast(U32).indirect(entries(look_list, j0, n))
+                within_half(v_w, j0, n), tab_w[:].bitcast(U32).indirect(entries(look_list, j0, n))
             )
 
         def look_up_scales(j0, n):
-            nc.vector.tensor_copy(v_s[:, j0 : j0 + n], tab_s[:].indirect(entries(look_list, j0, n)))
+            nc.vector.tensor_copy(within_half(v_s, j0, n), tab_s[:].indirect(entries(look_list, j0, n)))
 
         pieces = [(0, 0, QUARTER), (0, QUARTER, QUARTER), (0, HALF, HALF)]
         pieces = pieces + [(m, j0, HALF) for m in range(1, TILES) for j0 in (0, HALF)]
@@ -202,8 +205,8 @@ def tile_list_discharge_joint_page_kernel(
                 out=e,
                 lhsT=w1_w[:, cols(m, P)].bitcast(FP8X4),
                 lhsT_scale=w1_s[:, cols(m, P)],
-                rhs=words_of(j0, n).bitcast(FP8X4),
-                rhs_scale=v_s[:, j0 : j0 + n],
+                rhs=within_half(v_w, j0, n).bitcast(FP8X4),
+                rhs_scale=within_half(v_s, j0, n),
                 start=True,
                 stop=True,
             )
@@ -211,7 +214,10 @@ def tile_list_discharge_joint_page_kernel(
 
         def sine_and_gain(i, angle):
             m, j0, n = pieces[i]
-            sine = ring.tile([P, HALF], F32, name="sine", tag="sine")
+            if m > 0 and j0 == HALF:
+                sine = keep.tile([P, HALF], F32, name="last_sine", tag="slot%d" % (m % SLOTS))
+            else:
+                sine = ring.tile([P, HALF], F32, name="sine", tag="sine")
             nc.scalar.activation(sine[:, 0:n], angle, ACT.Sin, bias=half_pi[:], scale=-1.0)
             if j0 == 0:
                 h_tiles[m] = ring.tile([P, S], F32, name="h", tag="h", bufs=3)
@@ -223,10 +229,11 @@ def tile_list_discharge_joint_page_kernel(
             m, j0, n = pieces[i]
             e = first_product(i)
             if i == 0:
-                count = keep.tile([P, HALF], I32, name="first_count", tag="v_w1", align_bytes=64)[:, 0:n]
+                count = keep.tile([P, n], I32, name="first_count", tag="v_w1", align_bytes=64)[:]
+                rest = keep.tile([P, n], F32, name="first_rest", tag="v_s1", align_bytes=64)[:]
             else:
                 count = ring.tile([P, HALF], I32, name="signed_count", tag="count")[:, 0:n]
-            rest = ring.tile([P, HALF], F32, name="rest", tag="turns")[:, 0:n]
+                rest = ring.tile([P, HALF], F32, name="rest", tag="turns")[:, 0:n]
             size = folded[:, 0:n]
             nc.vector.tensor_scalar(count, e, shift[:, m : m + 1], 1.0 / (2 * math.pi), ALU.add, ALU.mult)
             nc.vector.scalar_tensor_tensor(rest, count, -2 * math.pi, e, ALU.mult, ALU.add)
@@ -268,15 +275,14 @@ def tile_list_discharge_joint_page_kernel(
                 pages[m][:].indirect(entries(offsets, j0, n)), values, factors[:, j0 : j0 + n], ALU.mult
             )
 
-        def pick(m, half, slot):
-            nc.vector.tensor_copy(
-                picked[:, cols(slot, HALF)], pages[m][:].indirect(entries(pick_list, half * HALF, HALF))
-            )
+        def pick(m, j0, n, place):
+            nc.vector.tensor_copy(picked[:, place : place + n], pages[m][:].indirect(entries(pick_list, j0, n)))
 
-        def cap(m, half, slot):
-            x_rows[m, half] = ring.tile([P, HALF], BF16, name="x_rows", tag="x_rows", bufs=6)
+        def cap(m, j0, n, place):
+            if j0 == 0:
+                x_rows[m] = keep.tile([P, S], BF16, name="x_rows", tag="slot%d" % ((m + 1) % SLOTS))
             nc.vector.tensor_tensor(
-                x_rows[m, half][:], picked[:, cols(slot, HALF)], ceils[m][:, cols(half, HALF)], ALU.min
+                x_rows[m][:, j0 : j0 + n], picked[:, place : place + n], ceils[m][:, j0 : j0 + n], ALU.min
             )
 
         def turn_x(m, half):
@@ -284,10 +290,10 @@ def tile_list_discharge_joint_page_kernel(
             b, q = divmod(m, 4)
             for jb in range(4):
                 nc.tensor.transpose(
-                    bank[:].bitcast(BF16)[:, cols(jb, P)], x_rows[m, half][:, cols(jb, P)], ident_bf[:]
+                    bank[:].bitcast(BF16)[:, cols(jb, P)], x_rows[m][:, cols(4 * half + jb, P)], ident_bf[:]
                 )
             if q == 0:
-                x_turned[half, b] = ring.tile([P, 4, 2, P], F32, name="x_turned", tag="x_turned", bufs=3)
+                x_turned[half, b] = ring.tile([P, 4, 2, P], F32, name="x_turned", tag="x_turned")
             nc.scalar.copy(
                 x_turned[half, b][:, :, :, cols(q, 32)],
                 bank[:, 0:QUARTER].rearrange("j (b p u) -> j b u p", b=4, u=2),
@@ -313,6 +319,14 @@ def tile_list_discharge_joint_page_kernel(
                 out=x_w[:, span].bitcast(FP8X4), scales=x_s[:, span], in_=grouped[:].bitcast(BF16)
             )
 
+        def early_picks(m):
+            place = (m % 2) * S
+            if m in LATE_TILES:
+                return ((0, HALF, place),)
+            if m == TILES - 1:
+                return ((0, HALF, place), (HALF, HALF, place + HALF))
+            return ((0, S, place),)
+
         def finish_piece(i):
             m, j0, n = pieces[i]
             if m == 0:
@@ -321,63 +335,69 @@ def tile_list_discharge_joint_page_kernel(
                 return
             if m > 0:
                 put(m, put_list, 0, S, h_tiles[m][:], wgs_sb)
-            halves = (0,) if m in LATE_TILES else (0, 1)
-            for half in halves:
-                pick(m, half, half)
-            for half in halves:
-                cap(m, half, half)
-            if m + 3 < TILES:
-                load_ceil(m + 3)
+            if m > 0:
+                for part in early_picks(m - 1):
+                    cap(m - 1, *part)
+            for part in early_picks(m):
+                pick(m, *part)
+            if 0 < m < TILES - 2:
+                load_ceil(m + 2)
             if m in (3, 5):
                 load_w2(m // 2 - 1)
             if m >= 6:
                 quantise_w2(m - 6)
             if m >= X_LAG:
-                done = m - X_LAG
-                for half in (0,) if done in LATE_TILES else (0, 1):
-                    turn_x(done, half)
+                for half in range(2):
+                    turn_x(m - X_LAG, half)
 
         quantise_w1(0)
         quantise_w1(1)
         look_up_scales(0, HALF)
-        look_up_scales(HALF, HALF)
         for i in range(FIRST_PIECES):
             if pieces[i][1] == HALF:
                 v_w[1] = keep.tile([P, HALF], U32, name="v_w1", tag="v_w1", align_bytes=64)
+                v_s[1] = keep.tile([P, HALF], U8, name="v_s1", tag="v_s1", align_bytes=64)
+                look_up_scales(HALF, HALF)
             look_up_words(pieces[i][1], pieces[i][2])
             reduce_on_vector(i)
-        quantise_w1(2)
         for i in range(FIRST_PIECES):
             finish_piece(i)
+        for i in range(FIRST_PIECES, PIPELINE_FROM):
+            stage_count(i)
+            stage_reduce(i)
+            stage_sine(i)
+            finish_piece(i)
+        quantise_w1(2)
+        quantise_w1(3)
         nc.vector.memset(w3_s[:].bitcast(I32), 0)
         load_scale_rows(w3_s, w3_scales)
-        for step in range(FIRST_PIECES, len(pieces) + 2):
+        for step in range(PIPELINE_FROM, len(pieces) + 2):
             if step < len(pieces):
                 m, j0, n = pieces[step]
                 if j0 == 0 and m + 2 < TILES:
                     quantise_w1(m + 2)
                 stage_count(step)
-            if FIRST_PIECES <= step - 1 < len(pieces):
+            if PIPELINE_FROM <= step - 1 < len(pieces):
                 stage_reduce(step - 1)
-            if FIRST_PIECES <= step - 2:
+            if PIPELINE_FROM <= step - 2:
                 stage_sine(step - 2)
                 finish_piece(step - 2)
+        for part in early_picks(TILES - 1):
+            cap(TILES - 1, *part)
         for m in range(TILES - X_LAG, TILES):
             turn_x(m, 0)
         for slot, m in enumerate(LATE_TILES):
-            pick(m, 1, slot)
+            pick(m, HALF, HALF, S + slot * HALF)
         for slot, m in enumerate(LATE_TILES):
-            cap(m, 1, slot)
+            cap(m, HALF, HALF, S + slot * HALF)
 
-        def second_stage(n, half):
-            bank = sum_banks[n % 2]
-            js = cols(half, HALF)
+        def second_product(n, half, bank, y):
             nc.tensor.matmul_mx(
                 out=bank[:],
                 lhsT=w3_w[:, cols(n, 2 * P)].bitcast(FP4X4),
                 lhsT_scale=w3_s[:, cols(n, P)],
                 rhs=v_w[half][:].bitcast(FP8X4),
-                rhs_scale=v_s[:, js],
+                rhs_scale=v_s[half][:],
                 start=True,
                 stop=False,
             )
@@ -392,19 +412,26 @@ def tile_list_discharge_joint_page_kernel(
                     start=False,
                     stop=b == PASSES - 1,
                 )
-            y = ring.tile([P, HALF], F32, name="y", tag="y", bufs=3)
-            nc.scalar.copy(y[:], bank[:])
-            put(n, final_list, half * HALF, HALF, y[:], wgo_sb)
+            nc.scalar.copy(y, bank[:])
+
+        def second_stage(n, halves):
+            y = ring.tile([P, S], F32, name="y", tag="h", bufs=3)
+            for half in halves:
+                bank = sum_banks[(n + half) % 2]
+                second_product(n, half, bank, y[:, cols(half, HALF)])
+            j0, count = halves[0] * HALF, len(halves) * HALF
+            put(n, final_list, j0, count, y[:, j0 : j0 + count], wgo_sb)
+            if halves[-1] == 1:
+                nc.sync.dma_start(out=out[cols(n, P), :], in_=pages[n][:])
 
         for n in range(TILES):
-            second_stage(n, 0)
+            second_stage(n, (0,) if n < SPLIT_TILES else (0, 1))
             if n == 0:
-                for m in LATE_TILES + (TILES - 1,):
+                for m in range(TILES - X_LAG, TILES):
                     turn_x(m, 1)
             if n % 2 == 0 and n // 2 + 2 < TILES // 2:
                 load_w2(n // 2 + 2)
             if n + 2 < TILES:
                 quantise_w2(n + 2)
-        for n in range(TILES):
-            second_stage(n, 1)
-            nc.sync.dma_start(out=out[cols(n, P), :], in_=pages[n][:])
+        for n in range(SPLIT_TILES):
+            second_stage(n, (1,))

@@ -28,8 +28,8 @@ FIRST_PIECES = 3
 PIPELINE_FROM = FIRST_PIECES + 2
 X_LAG = 3
 SLOTS = X_LAG + 1
-LATE_TILES = (5, 6)
-SPLIT_TILES = 2
+LATE_TILES = (4, 5, 6)
+SPLIT_TILES = 3
 
 
 def tile_list_discharge_joint_page_kernel(
@@ -97,9 +97,6 @@ def tile_list_discharge_joint_page_kernel(
         def load_weight(tile, rows_hbm):
             nc.sync.dma_start(out=tile, in_=rows_hbm.rearrange("(p t) c -> p t c", t=PACK))
 
-        vectors = keep.tile([2 * TILES, P], F32, name="vectors")
-        nc.sync.dma_start(out=vectors[0:TILES, :], in_=phase.rearrange("(m p) -> m p", p=P))
-        nc.sync.dma_start(out=vectors[TILES : 2 * TILES, :], in_=gain.rearrange("(m p) -> m p", p=P))
         landed = ring.tile([P, 2, T // 4], I32, name="landed", tag="raw")
         for upper in range(2):
             nc.sync.dma_start(
@@ -107,6 +104,9 @@ def tile_list_discharge_joint_page_kernel(
                 in_=tab_scales[0, 8 * upper : 8 * upper + 8, :].bitcast(I32).rearrange("(q r) n -> r q n", q=2),
             )
         nc.sync.dma_start(look_list[:], offs)
+        vectors = keep.tile([2 * TILES, P], F32, name="vectors")
+        nc.sync.dma_start(out=vectors[0:TILES, :], in_=phase.rearrange("(m p) -> m p", p=P))
+        nc.sync.dma_start(out=vectors[TILES : 2 * TILES, :], in_=gain.rearrange("(m p) -> m p", p=P))
         w1_first = keep.tile([P, PACK, QUARTER], F32, name="w1_first")
         load_weight(w1_first[:], w1[:, 0:QUARTER])
         nc.sync.dma_start(out=tab_w[:], in_=tab_words[0].rearrange("p n t -> p (n t)").bitcast(I32))
@@ -125,7 +125,7 @@ def tile_list_discharge_joint_page_kernel(
         ceils = {}
 
         def load_ceil(m):
-            ceils[m] = ring.tile([P, S], F32, name="ceil_sb", tag="ceil", bufs=3)
+            ceils[m] = ring.tile([P, S], F32, name="ceil_sb", tag="ceil", bufs=4)
             nc.sync.dma_start(out=ceils[m][:], in_=ceil[cols(m, P), :])
 
         load_ceil(0)
@@ -133,7 +133,7 @@ def tile_list_discharge_joint_page_kernel(
         w1_last = ring.tile([P, PACK, HALF], F32, name="w1_last", tag="raw")
         load_weight(w1_last[:], w1[:, HALF:H])
         for m in range(2, TILES):
-            if m < 4:
+            if m < 5:
                 load_ceil(m - 1)
             nc.sync.dma_start(out=pages[m][:], in_=page0[cols(m, P), :])
         nc.sync.dma_start(out=w3_w[:].bitcast(I32), in_=w3_words[0].bitcast(I32))
@@ -196,7 +196,7 @@ def tile_list_discharge_joint_page_kernel(
         pieces = [(0, 0, QUARTER), (0, QUARTER, QUARTER), (0, HALF, HALF)]
         pieces = pieces + [(m, j0, HALF) for m in range(1, TILES) for j0 in (0, HALF)]
         folded = kept("folded", 2 * HALF, F32)
-        turns, reduced, h_tiles, x_rows, x_turned = {}, {}, {}, {}, {}
+        turns, reduced, h_tiles, x_rows, x_turned, grouped_tiles = {}, {}, {}, {}, {}, {}
 
         def first_product(i):
             m, j0, n = pieces[i]
@@ -275,15 +275,13 @@ def tile_list_discharge_joint_page_kernel(
                 pages[m][:].indirect(entries(offsets, j0, n)), values, factors[:, j0 : j0 + n], ALU.mult
             )
 
-        def pick(m, j0, n, place):
-            nc.vector.tensor_copy(picked[:, place : place + n], pages[m][:].indirect(entries(pick_list, j0, n)))
+        def pick(m, j0, n, columns):
+            nc.vector.tensor_copy(columns, pages[m][:].indirect(entries(pick_list, j0, n)))
 
-        def cap(m, j0, n, place):
+        def cap(m, j0, n, columns):
             if j0 == 0:
                 x_rows[m] = keep.tile([P, S], BF16, name="x_rows", tag="slot%d" % ((m + 1) % SLOTS))
-            nc.vector.tensor_tensor(
-                x_rows[m][:, j0 : j0 + n], picked[:, place : place + n], ceils[m][:, j0 : j0 + n], ALU.min
-            )
+            nc.vector.tensor_tensor(x_rows[m][:, j0 : j0 + n], columns, ceils[m][:, j0 : j0 + n], ALU.min)
 
         def turn_x(m, half):
             bank = back_banks[0]
@@ -303,6 +301,7 @@ def tile_list_discharge_joint_page_kernel(
 
         def quantise_x(half, b):
             grouped = ring.tile([P, 2 * HALF], F32, name="grouped", tag="grouped", align_bytes=64)
+            grouped_tiles[half, b] = grouped
             for pair in range(2):
                 bank = word_banks[pair]
                 for jj in range(2):
@@ -320,12 +319,12 @@ def tile_list_discharge_joint_page_kernel(
             )
 
         def early_picks(m):
-            place = (m % 2) * S
+            side = picked[:, cols(m % 2, S)]
             if m in LATE_TILES:
-                return ((0, HALF, place),)
+                return ((0, HALF, side[:, 0:HALF]),)
             if m == TILES - 1:
-                return ((0, HALF, place), (HALF, HALF, place + HALF))
-            return ((0, S, place),)
+                return ((0, HALF, side[:, 0:HALF]), (HALF, HALF, side[:, HALF:S]))
+            return ((0, S, side),)
 
         def finish_piece(i):
             m, j0, n = pieces[i]
@@ -340,14 +339,14 @@ def tile_list_discharge_joint_page_kernel(
                     cap(m - 1, *part)
             for part in early_picks(m):
                 pick(m, *part)
-            if 0 < m < TILES - 2:
-                load_ceil(m + 2)
+            if 0 < m < TILES - 3:
+                load_ceil(m + 3)
             if m in (3, 5):
                 load_w2(m // 2 - 1)
             if m >= 6:
                 quantise_w2(m - 6)
             if m >= X_LAG:
-                for half in range(2):
+                for half in (0,) if m - X_LAG in LATE_TILES else (0, 1):
                     turn_x(m - X_LAG, half)
 
         quantise_w1(0)
@@ -386,10 +385,13 @@ def tile_list_discharge_joint_page_kernel(
             cap(TILES - 1, *part)
         for m in range(TILES - X_LAG, TILES):
             turn_x(m, 0)
-        for slot, m in enumerate(LATE_TILES):
-            pick(m, HALF, HALF, S + slot * HALF)
-        for slot, m in enumerate(LATE_TILES):
-            cap(m, HALF, HALF, S + slot * HALF)
+        for slot, m in enumerate(LATE_TILES[:-1]):
+            pick(m, HALF, HALF, picked[:, S + slot * HALF : S + (slot + 1) * HALF])
+        for slot, m in enumerate(LATE_TILES[:-1]):
+            cap(m, HALF, HALF, picked[:, S + slot * HALF : S + (slot + 1) * HALF])
+        last_columns = grouped_tiles[0, PASSES - 1][:, 0:HALF]
+        pick(LATE_TILES[-1], HALF, HALF, last_columns)
+        cap(LATE_TILES[-1], HALF, HALF, last_columns)
 
         def second_product(n, half, bank, y):
             nc.tensor.matmul_mx(
@@ -417,7 +419,10 @@ def tile_list_discharge_joint_page_kernel(
         def second_stage(n, halves):
             y = ring.tile([P, S], F32, name="y", tag="h", bufs=3)
             for half in halves:
-                bank = sum_banks[(n + half) % 2]
+                if (n, half) == (SPLIT_TILES - 1, 0):
+                    bank = word_banks[1]
+                else:
+                    bank = sum_banks[(n + half) % 2]
                 second_product(n, half, bank, y[:, cols(half, HALF)])
             j0, count = halves[0] * HALF, len(halves) * HALF
             put(n, final_list, j0, count, y[:, j0 : j0 + count], wgo_sb)
@@ -427,7 +432,7 @@ def tile_list_discharge_joint_page_kernel(
         for n in range(TILES):
             second_stage(n, (0,) if n < SPLIT_TILES else (0, 1))
             if n == 0:
-                for m in range(TILES - X_LAG, TILES):
+                for m in LATE_TILES + (TILES - 1,):
                     turn_x(m, 1)
             if n % 2 == 0 and n // 2 + 2 < TILES // 2:
                 load_w2(n // 2 + 2)

@@ -86,6 +86,8 @@ def tile_list_discharge_joint_page_kernel(
         nc.gpsimd.memset(rows[:], 0.0)
         make_identity(nc, ident[:])
         make_identity(nc, ident_bf[:])
+        warm = kept("warm", 1, F32)
+        nc.scalar.activation(warm[:], ident[:, 0:1], ACT.Sin)
 
         def load_scale_rows(plane, scales):
             for q in range(4):

import math
from contextlib import ExitStack

import concourse.mybir as mybir
from concourse.masks import make_identity

K, H, T, S, T2 = 512, 1024, 4096, 1024, 2048
FLOPS = 2 * S * H * (K + H + K)

F32 = mybir.dt.float32
BF16 = mybir.dt.bfloat16
I32 = mybir.dt.int32
U32 = mybir.dt.uint32
U16 = mybir.dt.uint16
U8 = mybir.dt.uint8
FP8X4 = mybir.dt.float8_e4m3fn_x4
FP4X4 = mybir.dt.float4_e2m1fn_x4
ACT = mybir.ActivationFunctionType
ALU = mybir.AluOpType

P = 128
PACK = 4
HALF = 512
QUARTER = 256
TILES = H // P
PASSES = H // (P * PACK)
FIRST_PIECES = 3
PIPELINE_FROM = FIRST_PIECES + 2
X_LAG = 3
SLOTS = X_LAG + 1
LATE_TILES = (4, 5, 6)
SPLIT_TILES = 3


def tile_list_discharge_joint_page_kernel(
    tc, tab_words, tab_scales, offs, offs2, offs3, offs4, w1, phase, gain,
    page0, wgs, ceil, w2, w3_words, w3_scales, wgo, out,
):
    nc = tc.nc
    with ExitStack() as ctx:
        keep = ctx.enter_context(tc.tile_pool(name="keep", bufs=1))
        ring = ctx.enter_context(tc.tile_pool(name="ring", bufs=2))
        psum = ctx.enter_context(tc.psum_pool(name="psum", bufs=1))

        def kept(name, cols, dtype):
            return keep.tile([P, cols], dtype, name=name, align_bytes=64)

        def entries(offsets, j0, n):
            return offsets[:, j0 // 16 : (j0 + n) // 16]

        def cols(i, width):
            return slice(i * width, (i + 1) * width)

        banks = [psum.tile([P, HALF], F32, name="bank%d" % i) for i in range(8)]
        sum_banks, turn_banks, back_banks, word_banks = banks[0:2], banks[2:4], banks[4:6], banks[6:8]

        look_list = keep.tile([P, S // 16], U16, name="look_list")
        put_list = keep.tile([P, S // 16], U16, name="put_list")
        pick_list = keep.tile([P, S // 16], U16, name="pick_list")
        final_list = keep.tile([P, S // 16], U16, name="final_list")
        tab_w = kept("tab_w", T, I32)
        tab_s = kept("tab_s", T, U8)
        v_w = {0: kept("v_w0", HALF, U32)}
        v_s = {0: kept("v_s0", HALF, U8)}
        w3_w = kept("w3_w", 2 * H, U8)
        w3_s = kept("w3_s", H, U8)
        w1_w = kept("w1_w", H, U32)
        w1_s = kept("w1_s", H, U8)
        w2_w = kept("w2_w", PASSES * H, U32)
        w2_s = kept("w2_s", PASSES * H, U8)
        x_w = kept("x_w", PASSES * S, U32)
        x_s = kept("x_s", PASSES * S, U8)
        rounded = kept("rounded", PACK * H, BF16)
        wgs_sb = kept("wgs_sb", S, F32)
        wgo_sb = kept("wgo_sb", S, F32)
        picked = kept("picked", 2 * S, F32)
        rows = kept("rows", P, F32)
        shift = kept("shift", TILES, F32)
        gains = kept("gains", TILES, F32)
        half_pi = kept("half_pi", 1, F32)
        ident = kept("ident", P, F32)
        ident_bf = kept("ident_bf", P, BF16)
        pages = [kept("page%d" % m, T2, F32) for m in range(TILES)]

        nc.vector.memset(tab_s[:].bitcast(I32), 0)
        nc.gpsimd.memset(rows[:], 0.0)
        make_identity(nc, ident[:])
        make_identity(nc, ident_bf[:])
        warm = kept("warm", 1, F32)
        nc.scalar.activation(warm[:], ident[:, 0:1], ACT.Sin)

        def load_scale_rows(plane, scales):
            for q in range(4):
                nc.sync.dma_start(
                    out=plane[32 * q : 32 * q + 4, :].bitcast(I32),
                    in_=scales[0, 4 * q : 4 * q + 4, :].bitcast(I32),
                )

        def load_weight(tile, rows_hbm):
            nc.sync.dma_start(out=tile, in_=rows_hbm.rearrange("(p t) c -> p t c", t=PACK))

        landed = ring.tile([P, 2, T // 4], I32, name="landed", tag="raw")
        for upper in range(2):
            nc.sync.dma_start(
                out=landed[64 * upper : 64 * upper + 4],
                in_=tab_scales[0, 8 * upper : 8 * upper + 8, :].bitcast(I32).rearrange("(q r) n -> r q n", q=2),
            )
        nc.sync.dma_start(look_list[:], offs)
        vectors = keep.tile([2 * TILES, P], F32, name="vectors")
        nc.sync.dma_start(out=vectors[0:TILES, :], in_=phase.rearrange("(m p) -> m p", p=P))
        nc.sync.dma_start(out=vectors[TILES : 2 * TILES, :], in_=gain.rearrange("(m p) -> m p", p=P))
        w1_first = keep.tile([P, PACK, QUARTER], F32, name="w1_first")
        load_weight(w1_first[:], w1[:, 0:QUARTER])
        nc.sync.dma_start(out=tab_w[:], in_=tab_words[0].rearrange("p n t -> p (n t)").bitcast(I32))
        nc.sync.dma_start(put_list[:], offs2)
        nc.scalar.copy(rows[0 : 2 * TILES, :], vectors[:])
        for q in range(4):
            upper, side = divmod(q, 2)
            nc.vector.tensor_copy(
                tab_s[32 * q : 32 * q + 4, :].bitcast(I32), landed[64 * upper : 64 * upper + 4, side, :]
            )
        w1_next = ring.tile([P, PACK, QUARTER], F32, name="w1_next", tag="raw")
        load_weight(w1_next[:], w1[:, QUARTER:HALF])
        nc.sync.dma_start(out=wgs_sb[:], in_=wgs)
        nc.sync.dma_start(out=pages[0][:], in_=page0[cols(0, P), :])
        nc.sync.dma_start(pick_list[:], offs3)
        ceils = {}

        def load_ceil(m):
            ceils[m] = ring.tile([P, S], F32, name="ceil_sb", tag="ceil", bufs=4)
            nc.sync.dma_start(out=ceils[m][:], in_=ceil[cols(m, P), :])

        load_ceil(0)
        nc.sync.dma_start(out=pages[1][:], in_=page0[cols(1, P), :])
        w1_last = ring.tile([P, PACK, HALF], F32, name="w1_last", tag="raw")
        load_weight(w1_last[:], w1[:, HALF:H])
        for m in range(2, TILES):
            if m < 5:
                load_ceil(m - 1)
            nc.sync.dma_start(out=pages[m][:], in_=page0[cols(m, P), :])
        nc.sync.dma_start(out=w3_w[:].bitcast(I32), in_=w3_words[0].bitcast(I32))
        nc.sync.dma_start(final_list[:], offs4)
        nc.sync.dma_start(out=wgo_sb[:], in_=wgo)

        nc.tensor.transpose(banks[7][:, 0:P], rows[:], ident[:])
        nc.vector.tensor_scalar_add(shift[:], banks[7][:, 0:TILES], -math.pi / 2)
        nc.vector.tensor_scalar_add(half_pi[:], banks[7][:, 2 * TILES : 2 * TILES + 1], math.pi / 2)
        nc.vector.tensor_copy(gains[:], banks[7][:, TILES : 2 * TILES])

        def round_weight(slot, raw):
            nc.scalar.copy(
                rounded[:, cols(slot, HALF)].rearrange("p (c i t) -> p c t i", i=4, t=PACK),
                raw.rearrange("p t (c i) -> p c t i", i=4),
            )

        def quantise_w1(m):
            if m < 2:
                raw = w1_first[:, :, cols(m, P)]
            elif m < 4:
                raw = w1_next[:, :, cols(m - 2, P)]
            else:
                raw = w1_last[:, :, cols(m - 4, P)]
            round_weight(m, raw)
            nc.vector.quantize_mx(
                out=w1_w[:, cols(m, P)].bitcast(FP8X4),
                scales=w1_s[:, cols(m, P)],
                in_=rounded[:, cols(m, HALF)],
            )

        w2_raw = {}

        def load_w2(pair):
            w2_raw[pair] = ring.tile([P, PASSES, PACK, QUARTER], F32, name="w2_raw", tag="raw")
            for b in range(PASSES):
                load_weight(w2_raw[pair][:, b], w2[cols(b, HALF), cols(pair, QUARTER)])

        def quantise_w2(n):
            slot = PASSES * (n % 4)
            for b in range(PASSES):
                round_weight(slot + b, w2_raw[n // 2][:, b, :, cols(n % 2, P)])
            nc.vector.quantize_mx(
                out=w2_w[:, cols(n, PASSES * P)].bitcast(FP8X4),
                scales=w2_s[:, cols(n, PASSES * P)],
                in_=rounded[:, slot * HALF : (slot + PASSES) * HALF],
            )

        def within_half(halves, j0, n):
            return halves[j0 // HALF][:, j0 % HALF : j0 % HALF + n]

        def look_up_words(j0, n):
            nc.vector.tensor_copy(
                within_half(v_w, j0, n), tab_w[:].bitcast(U32).indirect(entries(look_list, j0, n))
            )

        def look_up_scales(j0, n):
            nc.vector.tensor_copy(within_half(v_s, j0, n), tab_s[:].indirect(entries(look_list, j0, n)))

        pieces = [(0, 0, QUARTER), (0, QUARTER, QUARTER), (0, HALF, HALF)]
        pieces = pieces + [(m, j0, HALF) for m in range(1, TILES) for j0 in (0, HALF)]
        folded = kept("folded", 2 * HALF, F32)
        turns, reduced, h_tiles, x_rows, x_turned, grouped_tiles = {}, {}, {}, {}, {}, {}

        def first_product(i):
            m, j0, n = pieces[i]
            e = sum_banks[i % 2][:, 0:n]
            nc.tensor.matmul_mx(
                out=e,
                lhsT=w1_w[:, cols(m, P)].bitcast(FP8X4),
                lhsT_scale=w1_s[:, cols(m, P)],
                rhs=within_half(v_w, j0, n).bitcast(FP8X4),
                rhs_scale=within_half(v_s, j0, n),
                start=True,
                stop=True,
            )
            return e

        def sine_and_gain(i, angle):
            m, j0, n = pieces[i]
            if m > 0 and j0 == HALF:
                sine = keep.tile([P, HALF], F32, name="last_sine", tag="slot%d" % (m % SLOTS))
            else:
                sine = ring.tile([P, HALF], F32, name="sine", tag="sine")
            nc.scalar.activation(sine[:, 0:n], angle, ACT.Sin, bias=half_pi[:], scale=-1.0)
            if j0 == 0:
                h_tiles[m] = ring.tile([P, S], F32, name="h", tag="h", bufs=3)
            nc.scalar.activation(
                h_tiles[m][:, j0 : j0 + n], sine[:, 0:n], ACT.Copy, scale=gains[:, m : m + 1]
            )

        def reduce_on_vector(i):
            m, j0, n = pieces[i]
            e = first_product(i)
            if i == 0:
                count = keep.tile([P, n], I32, name="first_count", tag="v_w1", align_bytes=64)[:]
                rest = keep.tile([P, n], F32, name="first_rest", tag="v_s1", align_bytes=64)[:]
            else:
                count = ring.tile([P, HALF], I32, name="signed_count", tag="count")[:, 0:n]
                rest = ring.tile([P, HALF], F32, name="rest", tag="turns")[:, 0:n]
            size = folded[:, 0:n]
            nc.vector.tensor_scalar(count, e, shift[:, m : m + 1], 1.0 / (2 * math.pi), ALU.add, ALU.mult)
            nc.vector.scalar_tensor_tensor(rest, count, -2 * math.pi, e, ALU.mult, ALU.add)
            nc.scalar.activation(size, rest, ACT.Abs, bias=shift[:, m : m + 1])
            sine_and_gain(i, size)

        def stage_count(i):
            m, j0, n = pieces[i]
            e = first_product(i)
            size = folded[:, (i % 2) * HALF : (i % 2) * HALF + n]
            count = ring.tile([P, HALF], U32, name="count", tag="count")
            turns[i] = ring.tile([P, HALF], F32, name="turns", tag="turns")
            nc.scalar.activation(size, e, ACT.Abs, bias=shift[:, m : m + 1])
            nc.scalar.activation(count[:, 0:n], size, ACT.Copy, scale=1.0 / (2 * math.pi))
            nc.scalar.activation(turns[i][:, 0:n], count[:, 0:n], ACT.Copy, scale=-2 * math.pi)

        def stage_reduce(i):
            m, j0, n = pieces[i]
            bank = turn_banks[i % 2]
            size = folded[:, (i % 2) * HALF : (i % 2) * HALF + n]
            for blk in range(n // P):
                for src, first in ((size, True), (turns[i], False)):
                    nc.tensor.matmul(
                        bank[:, cols(blk, P)], lhsT=src[:, cols(blk, P)], rhs=ident[:],
                        is_transpose=True, start=first, stop=not first,
                    )
            reduced[i] = ring.tile([P, HALF], F32, name="reduced", tag="reduced")
            nc.scalar.activation(reduced[i][:, 0:n], bank[:, 0:n], ACT.Abs)

        def stage_sine(i):
            m, j0, n = pieces[i]
            bank = back_banks[i % 2]
            for blk in range(n // P):
                nc.tensor.transpose(bank[:, cols(blk, P)], reduced[i][:, cols(blk, P)], ident[:])
            sine_and_gain(i, bank[:, 0:n])

        def put(m, offsets, j0, n, values, factors):
            nc.vector.tensor_tensor(
                pages[m][:].indirect(entries(offsets, j0, n)), values, factors[:, j0 : j0 + n], ALU.mult
            )

        def pick(m, j0, n, columns):
            nc.vector.tensor_copy(columns, pages[m][:].indirect(entries(pick_list, j0, n)))

        def cap(m, j0, n, columns):
            if j0 == 0:
                x_rows[m] = keep.tile([P, S], BF16, name="x_rows", tag="slot%d" % ((m + 1) % SLOTS))
            nc.vector.tensor_tensor(x_rows[m][:, j0 : j0 + n], columns, ceils[m][:, j0 : j0 + n], ALU.min)

        def turn_x(m, half):
            bank = back_banks[0]
            b, q = divmod(m, 4)
            for jb in range(4):
                nc.tensor.transpose(
                    bank[:].bitcast(BF16)[:, cols(jb, P)], x_rows[m][:, cols(4 * half + jb, P)], ident_bf[:]
                )
            if q == 0:
                x_turned[half, b] = ring.tile([P, 4, 2, P], F32, name="x_turned", tag="x_turned")
            nc.scalar.copy(
                x_turned[half, b][:, :, :, cols(q, 32)],
                bank[:, 0:QUARTER].rearrange("j (b p u) -> j b u p", b=4, u=2),
            )
            if q == 3:
                quantise_x(half, b)

        def quantise_x(half, b):
            grouped = ring.tile([P, 2 * HALF], F32, name="grouped", tag="grouped", align_bytes=64)
            grouped_tiles[half, b] = grouped
            for pair in range(2):
                bank = word_banks[pair]
                for jj in range(2):
                    for u in range(2):
                        nc.tensor.transpose(
                            bank[:, cols(2 * jj + u, P)], x_turned[half, b][:, 2 * pair + jj, u, :], ident[:]
                        )
                nc.scalar.copy(
                    grouped[:, cols(pair, HALF)].rearrange("p (a j u) -> p a j u", a=2, u=2),
                    bank[:].rearrange("p (a u j) -> p a j u", a=2, u=2),
                )
            span = cols(PASSES * b + half, HALF)
            nc.vector.quantize_mx(
                out=x_w[:, span].bitcast(FP8X4), scales=x_s[:, span], in_=grouped[:].bitcast(BF16)
            )

        def early_picks(m):
            side = picked[:, cols(m % 2, S)]
            if m in LATE_TILES:
                return ((0, HALF, side[:, 0:HALF]),)
            if m == TILES - 1:
                return ((0, HALF, side[:, 0:HALF]), (HALF, HALF, side[:, HALF:S]))
            return ((0, S, side),)

        def finish_piece(i):
            m, j0, n = pieces[i]
            if m == 0:
                put(m, put_list, j0, n, h_tiles[m][:, j0 : j0 + n], wgs_sb)
            if j0 + n < S:
                return
            if m > 0:
                put(m, put_list, 0, S, h_tiles[m][:], wgs_sb)
            if m > 0:
                for part in early_picks(m - 1):
                    cap(m - 1, *part)
            for part in early_picks(m):
                pick(m, *part)
            if 0 < m < TILES - 3:
                load_ceil(m + 3)
            if m in (3, 5):
                load_w2(m // 2 - 1)
            if m >= 6:
                quantise_w2(m - 6)
            if m >= X_LAG:
                for half in (0,) if m - X_LAG in LATE_TILES else (0, 1):
                    turn_x(m - X_LAG, half)

        quantise_w1(0)
        quantise_w1(1)
        look_up_scales(0, HALF)
        for i in range(FIRST_PIECES):
            if pieces[i][1] == HALF:
                v_w[1] = keep.tile([P, HALF], U32, name="v_w1", tag="v_w1", align_bytes=64)
                v_s[1] = keep.tile([P, HALF], U8, name="v_s1", tag="v_s1", align_bytes=64)
                look_up_scales(HALF, HALF)
            look_up_words(pieces[i][1], pieces[i][2])
            reduce_on_vector(i)
        for i in range(FIRST_PIECES):
            finish_piece(i)
        for i in range(FIRST_PIECES, PIPELINE_FROM):
            stage_count(i)
            stage_reduce(i)
            stage_sine(i)
            finish_piece(i)
        quantise_w1(2)
        quantise_w1(3)
        nc.vector.memset(w3_s[:].bitcast(I32), 0)
        load_scale_rows(w3_s, w3_scales)
        for step in range(PIPELINE_FROM, len(pieces) + 2):
            if step < len(pieces):
                m, j0, n = pieces[step]
                if j0 == 0 and m + 2 < TILES:
                    quantise_w1(m + 2)
                stage_count(step)
            if PIPELINE_FROM <= step - 1 < len(pieces):
                stage_reduce(step - 1)
            if PIPELINE_FROM <= step - 2:
                stage_sine(step - 2)
                finish_piece(step - 2)
        for part in early_picks(TILES - 1):
            cap(TILES - 1, *part)
        for m in range(TILES - X_LAG, TILES):
            turn_x(m, 0)
        for slot, m in enumerate(LATE_TILES[:-1]):
            pick(m, HALF, HALF, picked[:, S + slot * HALF : S + (slot + 1) * HALF])
        for slot, m in enumerate(LATE_TILES[:-1]):
            cap(m, HALF, HALF, picked[:, S + slot * HALF : S + (slot + 1) * HALF])
        last_columns = grouped_tiles[0, PASSES - 1][:, 0:HALF]
        pick(LATE_TILES[-1], HALF, HALF, last_columns)
        cap(LATE_TILES[-1], HALF, HALF, last_columns)

        def second_product(n, half, bank, y):
            nc.tensor.matmul_mx(
                out=bank[:],
                lhsT=w3_w[:, cols(n, 2 * P)].bitcast(FP4X4),
                lhsT_scale=w3_s[:, cols(n, P)],
                rhs=v_w[half][:].bitcast(FP8X4),
                rhs_scale=v_s[half][:],
                start=True,
                stop=False,
            )
            for b in range(PASSES):
                span = cols(PASSES * b + half, HALF)
                nc.tensor.matmul_mx(
                    out=bank[:],
                    lhsT=w2_w[:, cols(PASSES * n + b, P)].bitcast(FP8X4),
                    lhsT_scale=w2_s[:, cols(PASSES * n + b, P)],
                    rhs=x_w[:, span].bitcast(FP8X4),
                    rhs_scale=x_s[:, span],
                    start=False,
                    stop=b == PASSES - 1,
                )
            nc.scalar.copy(y, bank[:])

        def second_stage(n, halves):
            y = ring.tile([P, S], F32, name="y", tag="h", bufs=3)
            for half in halves:
                if (n, half) == (SPLIT_TILES - 1, 0):
                    bank = word_banks[1]
                else:
                    bank = sum_banks[(n + half) % 2]
                second_product(n, half, bank, y[:, cols(half, HALF)])
            j0, count = halves[0] * HALF, len(halves) * HALF
            put(n, final_list, j0, count, y[:, j0 : j0 + count], wgo_sb)
            if halves[-1] == 1:
                nc.sync.dma_start(out=out[cols(n, P), :], in_=pages[n][:])

        for n in range(TILES):
            second_stage(n, (0,) if n < SPLIT_TILES else (0, 1))
            if n == 0:
                for m in LATE_TILES + (TILES - 1,):
                    turn_x(m, 1)
            if n % 2 == 0 and n // 2 + 2 < TILES // 2:
                load_w2(n // 2 + 2)
            if n + 2 < TILES:
                quantise_w2(n + 2)
        for n in range(SPLIT_TILES):
            second_stage(n, (1,))
